import numpy as np
import ml_dtypes


def mxq(x, axis, fmt="e4m3"):
    dtype, down = {"e4m3": (ml_dtypes.float8_e4m3fn, 7), "e5m2": (ml_dtypes.float8_e5m2, 14)}[fmt]
    v = np.moveaxis(np.asarray(x, np.float32).astype(ml_dtypes.bfloat16).astype(np.float64), axis, -1)
    blocks = v.reshape(v.shape[:-1] + (-1, 32))
    amax = np.abs(blocks).max(-1, keepdims=True)
    byte = np.maximum(np.where(amax > 0, np.frexp(amax)[1] - 1 + 127, 0) - down, 1)
    scale = np.exp2(byte - 127.0)
    codes = (blocks / scale).astype(np.float32).astype(dtype).astype(np.float64)
    return np.moveaxis((codes * scale).reshape(v.shape), -1, axis)


WIDE = False


def mx_kscale(k):
    if not WIDE:
        return np.ones(k)
    levels = np.array([10, -10, 5, -5, 0])
    if k % 512:
        return np.exp2(np.random.permutation(np.resize(levels, k // 32))).repeat(32)
    a = np.empty((k // 512, 16))
    for p in range(k // 512):
        a[p, :8] = np.random.permutation(np.resize(levels, 8))
        for g in range(8):
            far = levels[np.abs(levels - a[p, g]) >= 10]
            a[p, g + 8] = far[np.random.randint(len(far))]
    return np.exp2(a.ravel()).repeat(32)


def f64(x):
    return np.asarray(x).astype(np.float64)


def striped(idx):
    return np.tile(idx.reshape(-1, 16).T, (8, 1)).astype(np.uint16)


def unstriped(offs):
    return offs[:16].T.reshape(-1).astype(np.int64)


def striped8(idx):
    return np.concatenate([x.reshape(-1, 16).T for x in idx]).astype(np.uint16)


def runs(offs, k):
    lists = np.stack([offs[16 * r : 16 * r + 16].T.reshape(-1) for r in range(8)]).astype(np.int64)
    return lists[np.arange(k) % 512 // 64]


def pack_weight(w):
    k, n = w.shape
    w = f64(np.asarray(w, np.float32).astype(ml_dtypes.bfloat16)).reshape(k // 32, 32, n)
    amax = np.abs(w).max(1)
    byte = np.clip(np.where(amax > 0, np.frexp(amax)[1] - 1 + 127 - 7, 1), 1, 254)
    scaled = (w * np.exp2(127.0 - byte)[:, None, :]).reshape(k, n).astype(np.float32)
    words = np.ascontiguousarray(scaled.reshape(k // 512, 128, 4, n).transpose(0, 1, 3, 2)).astype(ml_dtypes.float8_e4m3fn).view(np.uint8)
    return words, np.ascontiguousarray(byte.astype(np.uint8).reshape(k // 512, 16, n))


def unpack_weight(words, scales):
    g, p, n, _ = words.shape
    vals = np.ascontiguousarray(words).view(ml_dtypes.float8_e4m3fn).astype(np.float64) * np.repeat(np.exp2(scales.astype(np.float64) - 127.0), 8, axis=1)[..., None]
    return vals.transpose(0, 1, 3, 2).reshape(g * 512, n)


E2M1 = np.array([0.0, 0.5, 1.0, 1.5, 2.0, 3.0, 4.0, 6.0, -0.0, -0.5, -1.0, -1.5, -2.0, -3.0, -4.0, -6.0])


def pack_fp4(w):
    k, n = w.shape
    w = f64(np.asarray(w, np.float32).astype(ml_dtypes.bfloat16)).reshape(k // 32, 32, n)
    amax = np.abs(w).max(1)
    mant, ex = np.frexp(amax / 6.0)
    byte = np.clip(np.where(amax > 0, np.where(mant > 0.5, ex, ex - 1) + 127, 1), 1, 254)
    scaled = (w * np.exp2(127.0 - byte)[:, None, :]).reshape(k, n).astype(np.float32)
    c = np.ascontiguousarray(scaled.reshape(k // 512, 128, 4, n).transpose(0, 1, 3, 2)).astype(ml_dtypes.float4_e2m1fn).view(np.uint8) & 0xF
    words = (c[..., 0::2] | (c[..., 1::2] << 4)).reshape(k // 512, 128, 2 * n)
    return np.ascontiguousarray(words), np.ascontiguousarray(byte.astype(np.uint8).reshape(k // 512, 16, n))


def unpack_fp4(words, scales):
    g, _, n = scales.shape
    words = np.ascontiguousarray(words).reshape(g, 128, n, 2)
    nib = np.empty((g, 128, n, 4), np.uint8)
    nib[..., 0::2] = words & 0xF
    nib[..., 1::2] = words >> 4
    vals = E2M1[nib] * np.repeat(np.exp2(scales.astype(np.float64) - 127.0), 8, axis=1)[..., None]
    return vals.transpose(0, 1, 3, 2).reshape(g * 512, n)


def planes(y):
    n, m = y.shape
    v = y.astype(np.float32).astype(ml_dtypes.bfloat16).astype(np.float64).reshape(n // 32, 32, m)
    top = np.abs(v).max(1)
    byte = np.clip(np.where(top > 0, np.frexp(top)[1] - 1 + 127 - 7, 1), 1, 254)
    codes = (v * np.exp2(127.0 - byte)[:, None, :]).reshape(n, m).astype(np.float32).astype(ml_dtypes.float8_e4m3fn).view(np.uint8)
    words = codes.reshape(n // 512, 128, 4, m).transpose(0, 1, 3, 2)
    return np.ascontiguousarray(words), np.ascontiguousarray(byte.astype(np.uint8).reshape(n // 512, 16, m))


K, T, S, N, H = 512, 2048, 512, 512, 512


def setup_inputs():
    n = np.random.standard_normal
    s = mx_kscale(K)[:, None]
    u = mx_kscale(H)
    packed_xT = pack_weight(n((K, T)) * s)
    packed_w1 = pack_fp4(n((K, H)) / np.sqrt(K) / s)
    packed_w2 = pack_fp4(n((H, N)) / np.sqrt(H) / u[:, None])
    return {
        "x_words": packed_xT[0],
        "x_scales": packed_xT[1],
        "w1_words": packed_w1[0],
        "w1_scales": packed_w1[1],
        "gn": (np.random.uniform(0.5, 1.5, (H, 1)) * u[:, None]).astype(np.float32),
        "w2_words": packed_w2[0],
        "w2_scales": packed_w2[1],
        "offs": striped(np.random.permutation(T)[:S]),
        "n1": striped8(np.stack([np.random.permutation(S) for _ in range(8)])),
        "n2": striped8(np.stack([np.random.permutation(S) for _ in range(8)])),
        "n3": striped8(np.stack([np.random.permutation(S) for _ in range(8)])),
    }


def reference(x_words, x_scales, w1_words, w1_scales, gn, w2_words, w2_scales, offs, n1, n2, n3):
    xq = unpack_weight(x_words, x_scales)[:, unstriped(offs)]
    y = unpack_fp4(w1_words, w1_scales).T @ xq
    z = f64(gn) * (y / (np.abs(y[np.arange(H)[:, None], runs(n1, H)]) + 0.5))
    h = unpack_fp4(w2_words, w2_scales).T @ mxq(z, 0, "e4m3")
    out_0 = 0.75 * (h * (y[np.arange(H)[:, None], runs(n3, H)]) - ((h[np.arange(N)[:, None], runs(n2, N)]) * y))
    return (out_0,) + planes(out_0)

@@ -1,0 +1,263 @@
+from contextlib import ExitStack
+
+import concourse.mybir as mybir
+
+F32 = mybir.dt.float32
+BF16 = mybir.dt.bfloat16
+I32 = mybir.dt.int32
+U32 = mybir.dt.uint32
+U16 = mybir.dt.uint16
+U8 = mybir.dt.uint8
+FP8X4 = mybir.dt.float8_e4m3fn_x4
+FP4X4 = mybir.dt.float4_e2m1fn_x4
+ACT = mybir.ActivationFunctionType
+ALU = mybir.AluOpType
+
+P = 128
+PACK = 4
+T = 2048
+S = 512
+LIST_ROWS = 16
+FLOPS = 2 * 2 * 512 * 512 * 512
+
+HALVES = [(0, 256), (256, 256)]
+Z_CHUNKS = [(0, 256), (256, 128), (384, 128)]
+OUT_CHUNKS = [(0, 256), (256, 128), (384, 128)]
+ABS_ON_SCALAR = (0, 2)
+EARLY_N3 = (1,)
+
+
+def entries(lists, first, width):
+    return lists[:, first // LIST_ROWS : (first + width) // LIST_ROWS]
+
+
+def planes_in_pairs(planes, first, width):
+    return planes[:, :, first : first + width].rearrange("p t (c i) -> p c t i", i=2)
+
+
+def words_in_pairs(grouped):
+    return grouped[:].rearrange("p (c i) t -> p c t i", i=2)
+
+
+def load_scale_rows(queues, plane, scales):
+    for q in range(4):
+        queues[q % len(queues)].dma_start(out=plane[32 * q : 32 * q + 4, :].bitcast(I32), in_=scales[0, 4 * q : 4 * q + 4, :].bitcast(I32))
+
+
+def tile_picked_skipcrossbnorm_none_po_kernel(
+    tc, x_words, x_scales, w1_words, w1_scales, gn, w2_words, w2_scales, offs, n1, n2, n3, out_0, out_1, out_2
+):
+    nc = tc.nc
+    with ExitStack() as ctx:
+        sb = ctx.enter_context(tc.tile_pool(name="sb", bufs=1))
+        ps = ctx.enter_context(tc.psum_pool(name="ps", bufs=1))
+
+        offs_sb = sb.tile([P, S // LIST_ROWS], U16, name="offs_sb")
+        n1_sb = sb.tile([P, S // LIST_ROWS], U16, name="n1_sb")
+        n2_sb = sb.tile([P, S // LIST_ROWS], U16, name="n2_sb")
+        n3_sb = sb.tile([P, S // LIST_ROWS], U16, name="n3_sb")
+        xw = sb.tile([P, T], I32, name="xw", align_bytes=64)
+        xs = sb.tile([P, T], U8, name="xs", align_bytes=64)
+        w1w = sb.tile([P, 2 * S], U8, name="w1w", tag="w_words", align_bytes=64)
+        w1s = sb.tile([P, S], U8, name="w1s", align_bytes=64)
+        w2s = sb.tile([P, S], U8, name="w2s", align_bytes=64)
+        gain = sb.tile([P, PACK], F32, name="gain")
+        half = sb.tile([P, 1], F32, name="half")
+        zero = sb.tile([P, 1], F32, name="zero")
+
+        nc.vector.memset(xs[:].bitcast(I32), 0)
+        nc.gpsimd.memset(w1s[:].bitcast(I32), 0)
+        nc.vector.memset(half[:], 0.5)
+        nc.vector.memset(w2s[:].bitcast(I32), 0)
+
+        nc.sync.dma_start(offs_sb[:], offs)
+        nc.sync.dma_start(out=xw[:], in_=x_words[0].rearrange("p n t -> p (n t)").bitcast(I32))
+        nc.scalar.dma_start(out=w1w[:].bitcast(I32), in_=w1_words[0].bitcast(I32))
+        load_scale_rows((nc.scalar, nc.sync), xs, x_scales)
+        load_scale_rows((nc.scalar, nc.sync), w1s, w1_scales)
+        nc.sync.dma_start(n1_sb[:], n1)
+        nc.sync.dma_start(n3_sb[:], n3)
+        nc.sync.dma_start(n2_sb[:], n2)
+        nc.gpsimd.dma_start(out=gain[:], in_=gn.rearrange("(p t) o -> p (t o)", t=PACK))
+        load_scale_rows((nc.sync,), w2s, w2_scales)
+
+        nc.scalar.activation(out=zero[:], in_=half[:], func=ACT.Ln, scale=2.0)
+
+        def deal_words(words, name):
+            dealt = sb.tile([P, 2 * S], U8, name=name, align_bytes=64)
+            nc.vector.tensor_copy(
+                out=dealt[:].rearrange("p (t m b) -> p t m b", t=PACK, b=2),
+                in_=words[:].rearrange("p (m t b) -> p t m b", t=PACK, b=2),
+            )
+            return dealt
+
+        def deal_scales(scales, name):
+            dealt = sb.tile([P, S], U8, name=name, align_bytes=64)
+            nc.vector.tensor_copy(
+                out=dealt[:].rearrange("p (t m) -> p t m", t=PACK),
+                in_=scales[:].rearrange("p (m t) -> p t m", t=PACK),
+            )
+            return dealt
+
+        def product(bank, weights, t, codes, scales):
+            nc.tensor.matmul_mx(
+                out=bank,
+                lhsT=weights[0][:, 2 * P * t : 2 * P * (t + 1)].bitcast(FP4X4),
+                lhsT_scale=weights[1][:, P * t : P * (t + 1)],
+                rhs=codes.bitcast(FP8X4),
+                rhs_scale=scales,
+                start=True,
+                stop=True,
+            )
+
+        w1_dealt_words = deal_words(w1w, "w1_dw")
+        w2w = sb.tile([P, 2 * S], U8, name="w2w", tag="w_words", align_bytes=64)
+        nc.sync.dma_start(out=w2w[:].bitcast(I32), in_=w2_words[0].bitcast(I32))
+        xgs = sb.tile([P, S], U8, name="xgs", align_bytes=64)
+        xg = sb.tile([P, S], I32, name="xg", align_bytes=64)
+        nc.vector.tensor_copy(out=xgs[:], in_=xs[:].indirect(offs_sb[:]))
+        for first, width in HALVES:
+            nc.vector.tensor_copy(
+                out=xg[:, first : first + width].bitcast(U32),
+                in_=xw[:].bitcast(U32).indirect(entries(offs_sb, first, width)),
+            )
+        w1 = (w1_dealt_words, deal_scales(w1s, "w1_ds"))
+
+        y_ps = [ps.tile([P, S], F32, name="y_ps%d" % t, tag="bank%d" % t) for t in range(PACK)]
+        for pair in ((0, 1), (2, 3)):
+            for first, width in HALVES:
+                for t in pair:
+                    cols = slice(first, first + width)
+                    product(y_ps[t][:, cols], w1, t, xg[:, cols], xgs[:, cols])
+
+        y = [sb.tile([P, S], F32, name="y%d" % t) for t in range(PACK)]
+        size = [sb.tile([P, S], F32, name="size%d" % t) for t in range(PACK)]
+        logs = [sb.tile([P, S], F32, name="logs%d" % t) for t in range(PACK)]
+        for t in range(PACK):
+            if t in ABS_ON_SCALAR:
+                nc.scalar.activation(out=size[t][:], in_=y_ps[t][:], func=ACT.Abs, bias=zero[:])
+            else:
+                nc.vector.tensor_copy(out=y[t][:], in_=y_ps[t][:])
+                nc.vector.scalar_tensor_tensor(
+                    out=size[t][:], in0=y_ps[t][:], scalar=-1.0, in1=y[t][:], op0=ALU.mult, op1=ALU.max
+                )
+        for t in (0, 2, 1, 3):
+            nc.scalar.activation(out=logs[t][:], in_=size[t][:], func=ACT.Ln, bias=half[:])
+        for t in ABS_ON_SCALAR:
+            nc.vector.tensor_copy(out=y[t][:], in_=y_ps[t][:])
+        w2 = (deal_words(w2w, "w2_dw"), deal_scales(w2s, "w2_ds"))
+
+        yg = sb.tile([P, PACK, S], F32, name="yg")
+        for t in range(PACK):
+            nc.vector.tensor_scalar(
+                out=yg[:, t, :], in0=y[t][:], scalar1=gain[:, t : t + 1], scalar2=None, op0=ALU.mult
+            )
+
+        y3 = sb.tile([P, PACK, S], F32, name="y_at_n3")
+
+        def fetch_y3(t):
+            for first, width in HALVES:
+                nc.vector.tensor_copy(
+                    out=y3[:, t, first : first + width], in_=y[t][:].indirect(entries(n3_sb, first, width))
+                )
+
+        inv = sb.tile([P, PACK, S], F32, name="inv")
+        zw = sb.tile([P, S], I32, name="zw", align_bytes=64)
+        zs = sb.tile([P, S], U8, name="zs", align_bytes=64)
+        h = [sb.tile([P, S], F32, name="h%d" % t) for t in range(PACK)]
+        for t in EARLY_N3:
+            fetch_y3(t)
+        for c, (first, width) in enumerate(Z_CHUNKS):
+            cols = slice(first, first + width)
+            for t in range(PACK):
+                nc.scalar.activation(
+                    out=inv[:, t, cols],
+                    in_=logs[t][:].indirect(entries(n1_sb, first, width)),
+                    func=ACT.Exp,
+                    scale=-1.0,
+                )
+            zb = sb.tile([P, width, PACK], BF16, name="zb%d" % c, align_bytes=64)
+            nc.vector.tensor_tensor(
+                out=words_in_pairs(zb),
+                in0=planes_in_pairs(yg, first, width),
+                in1=planes_in_pairs(inv, first, width),
+                op=ALU.mult,
+            )
+            nc.vector.quantize_mx(
+                out=zw[:, cols].bitcast(FP8X4), scales=zs[:, cols], in_=zb[:].rearrange("p c t -> p (c t)")
+            )
+
+        for c, (first, width) in enumerate(Z_CHUNKS):
+            cols = slice(first, first + width)
+            if c == 0:
+                pairs = [ps.tile([P, 2, width], F32, name="h_ps0%d" % u, tag="bank%d" % (4 + u)) for u in range(2)]
+                banks = [pairs[t // 2][:, t % 2, :] for t in range(PACK)]
+            elif c == 1:
+                pairs = [ps.tile([P, 2, width], F32, name="h_ps1%d" % u, tag="bank%d" % (6 + u)) for u in range(2)]
+                banks = [pairs[t // 2][:, t % 2, :] for t in range(PACK)]
+            else:
+                singles = [ps.tile([P, width], F32, name="h_ps2%d" % t, tag="bank%d" % t) for t in range(PACK)]
+                banks = [single[:] for single in singles]
+            for t in range(PACK):
+                product(banks[t], w2, t, zw[:, cols], zs[:, cols])
+            for t in range(PACK):
+                nc.scalar.activation(out=h[t][:, cols], in_=banks[t], func=ACT.Copy, scale=0.75)
+
+        left = sb.tile([P, PACK, S], F32, name="left")
+        right = sb.tile([P, PACK, S], F32, name="right")
+        res = sb.tile([P, PACK, S], F32, name="res")
+        ow = sb.tile([P, S], I32, name="ow", align_bytes=64)
+        osc = sb.tile([P, S], U8, name="osc", align_bytes=64)
+        out_rows = out_0.rearrange("(p t) j -> p t j", t=PACK)
+        out_words = out_1[0].rearrange("p n t -> p (n t)").bitcast(I32)
+
+        for first, width in Z_CHUNKS:
+            cols = slice(first, first + width)
+            for t in range(PACK):
+                if t in EARLY_N3:
+                    fetched = y3[:, t, cols]
+                else:
+                    fetched = y[t][:].indirect(entries(n3_sb, first, width))
+                nc.vector.tensor_tensor(out=left[:, t, cols], in0=fetched, in1=h[t][:, cols], op=ALU.mult)
+
+        waiting = []
+
+        def quantize_out(grouped, cols):
+            nc.vector.quantize_mx(
+                out=ow[:, cols].bitcast(FP8X4), scales=osc[:, cols], in_=grouped[:].rearrange("p c t -> p (c t)")
+            )
+            nc.sync.dma_start(out=out_words[:, cols], in_=ow[:, cols])
+
+        for c, (first, width) in enumerate(OUT_CHUNKS):
+            cols = slice(first, first + width)
+            last = c == len(OUT_CHUNKS) - 1
+            for t in range(PACK):
+                nc.vector.tensor_tensor(
+                    out=right[:, t, cols],
+                    in0=h[t][:].indirect(entries(n2_sb, first, width)),
+                    in1=y[t][:, cols],
+                    op=ALU.mult,
+                )
+            for grouped, earlier in waiting:
+                quantize_out(grouped, earlier)
+            waiting.clear()
+            ob = sb.tile([P, width, PACK], BF16, name="ob%d" % c, align_bytes=64)
+            if last:
+                nc.vector.tensor_tensor(
+                    out=words_in_pairs(ob),
+                    in0=planes_in_pairs(left, first, width),
+                    in1=planes_in_pairs(right, first, width),
+                    op=ALU.subtract,
+                )
+            nc.vector.tensor_tensor(out=res[:, :, cols], in0=left[:, :, cols], in1=right[:, :, cols], op=ALU.subtract)
+            nc.sync.dma_start(out=out_rows[:, :, cols], in_=res[:, :, cols])
+            if last:
+                quantize_out(ob, cols)
+            else:
+                nc.scalar.copy(out=words_in_pairs(ob), in_=planes_in_pairs(res, first, width))
+                waiting.append((ob, cols))
+        for q in range(4):
+            queue = nc.scalar if q % 2 else nc.sync
+            queue.dma_start(
+                out=out_2[0, 4 * q : 4 * q + 4, :].bitcast(I32), in_=osc[32 * q : 32 * q + 4, :].bitcast(I32)
+            )

@@ -23,8 +23,7 @@ FLOPS = 2 * 2 * 512 * 512 * 512
 HALVES = [(0, 256), (256, 256)]
 Z_CHUNKS = [(0, 256), (256, 128), (384, 128)]
 OUT_CHUNKS = [(0, 256), (256, 128), (384, 128)]
-ABS_ON_SCALAR = (0, 2)
-EARLY_N3 = (1,)
+EARLY_N3 = (0, 1, 2)
 
 
 def entries(lists, first, width):
@@ -113,8 +112,8 @@ def tile_picked_skipcrossbnorm_none_po_kernel(
         w1_dealt_words = deal_words(w1w, "w1_dw")
         w2w = sb.tile([P, 2 * S], U8, name="w2w", tag="w_words", align_bytes=64)
         nc.sync.dma_start(out=w2w[:].bitcast(I32), in_=w2_words[0].bitcast(I32))
-        xgs = sb.tile([P, S], U8, name="xgs", align_bytes=64)
-        xg = sb.tile([P, S], I32, name="xg", align_bytes=64)
+        xgs = sb.tile([P, S], U8, name="picked_scales", align_bytes=64)
+        xg = sb.tile([P, S], I32, name="picked_words", align_bytes=64)
         nc.vector.tensor_copy(out=xgs[:], in_=xs[:].indirect(offs_sb[:]))
         for first, width in HALVES:
             nc.vector.tensor_copy(
@@ -134,24 +133,18 @@ def tile_picked_skipcrossbnorm_none_po_kernel(
         size = [sb.tile([P, S], F32, name="size%d" % t) for t in range(PACK)]
         logs = [sb.tile([P, S], F32, name="logs%d" % t) for t in range(PACK)]
         for t in range(PACK):
-            if t in ABS_ON_SCALAR:
-                nc.scalar.activation(out=size[t][:], in_=y_ps[t][:], func=ACT.Abs, bias=zero[:])
-            else:
-                nc.vector.tensor_copy(out=y[t][:], in_=y_ps[t][:])
-                nc.vector.scalar_tensor_tensor(
-                    out=size[t][:], in0=y_ps[t][:], scalar=-1.0, in1=y[t][:], op0=ALU.mult, op1=ALU.max
-                )
-        for t in (0, 2, 1, 3):
-            nc.scalar.activation(out=logs[t][:], in_=size[t][:], func=ACT.Ln, bias=half[:])
-        for t in ABS_ON_SCALAR:
+            nc.scalar.activation(out=size[t][:], in_=y_ps[t][:], func=ACT.Abs, bias=zero[:])
             nc.vector.tensor_copy(out=y[t][:], in_=y_ps[t][:])
-        w2 = (deal_words(w2w, "w2_dw"), deal_scales(w2s, "w2_ds"))
+        for t in range(PACK):
+            nc.scalar.activation(out=logs[t][:], in_=size[t][:], func=ACT.Ln, bias=half[:])
 
         yg = sb.tile([P, PACK, S], F32, name="yg")
         for t in range(PACK):
             nc.vector.tensor_scalar(
                 out=yg[:, t, :], in0=y[t][:], scalar1=gain[:, t : t + 1], scalar2=None, op0=ALU.mult
             )
+
+        w2 = (deal_words(w2w, "picked_words"), deal_scales(w2s, "picked_scales"))
 
         y3 = sb.tile([P, PACK, S], F32, name="y_at_n3")
 
@@ -222,11 +215,11 @@ def tile_picked_skipcrossbnorm_none_po_kernel(
 
         waiting = []
 
-        def quantize_out(grouped, cols):
+        def quantize_out(grouped, cols, queue):
             nc.vector.quantize_mx(
                 out=ow[:, cols].bitcast(FP8X4), scales=osc[:, cols], in_=grouped[:].rearrange("p c t -> p (c t)")
             )
-            nc.sync.dma_start(out=out_words[:, cols], in_=ow[:, cols])
+            queue.dma_start(out=out_words[:, cols], in_=ow[:, cols])
 
         for c, (first, width) in enumerate(OUT_CHUNKS):
             cols = slice(first, first + width)
@@ -239,7 +232,7 @@ def tile_picked_skipcrossbnorm_none_po_kernel(
                     op=ALU.mult,
                 )
             for grouped, earlier in waiting:
-                quantize_out(grouped, earlier)
+                quantize_out(grouped, earlier, nc.sync)
             waiting.clear()
             ob = sb.tile([P, width, PACK], BF16, name="ob%d" % c, align_bytes=64)
             if last:
@@ -249,15 +242,14 @@ def tile_picked_skipcrossbnorm_none_po_kernel(
                     in1=planes_in_pairs(right, first, width),
                     op=ALU.subtract,
                 )
+                quantize_out(ob, cols, nc.scalar)
+                for q in range(4):
+                    queue = nc.scalar if q % 2 else nc.sync
+                    queue.dma_start(
+                        out=out_2[0, 4 * q : 4 * q + 4, :].bitcast(I32), in_=osc[32 * q : 32 * q + 4, :].bitcast(I32)
+                    )
             nc.vector.tensor_tensor(out=res[:, :, cols], in0=left[:, :, cols], in1=right[:, :, cols], op=ALU.subtract)
             nc.sync.dma_start(out=out_rows[:, :, cols], in_=res[:, :, cols])
-            if last:
-                quantize_out(ob, cols)
-            else:
+            if not last:
                 nc.scalar.copy(out=words_in_pairs(ob), in_=planes_in_pairs(res, first, width))
                 waiting.append((ob, cols))
-        for q in range(4):
-            queue = nc.scalar if q % 2 else nc.sync
-            queue.dma_start(
-                out=out_2[0, 4 * q : 4 * q + 4, :].bitcast(I32), in_=osc[32 * q : 32 * q + 4, :].bitcast(I32)
-            )

@@ -23,7 +23,7 @@ FLOPS = 2 * 2 * 512 * 512 * 512
 HALVES = [(0, 256), (256, 256)]
 Z_CHUNKS = [(0, 256), (256, 128), (384, 128)]
 OUT_CHUNKS = [(0, 256), (256, 128), (384, 128)]
-EARLY_N3 = (0, 1, 2)
+EARLY_N3 = (0, 1, 2, 3)
 
 
 def entries(lists, first, width):
@@ -140,8 +140,8 @@ def tile_picked_skipcrossbnorm_none_po_kernel(
 
         yg = sb.tile([P, PACK, S], F32, name="yg")
         for t in range(PACK):
-            nc.vector.tensor_scalar(
-                out=yg[:, t, :], in0=y[t][:], scalar1=gain[:, t : t + 1], scalar2=None, op0=ALU.mult
+            nc.gpsimd.tensor_scalar(
+                out=yg[:, t, :], in0=y[t][:], scalar1=gain[:, t : t + 1], scalar2=0.0, op0=ALU.mult, op1=ALU.add
             )
 
         w2 = (deal_words(w2w, "picked_words"), deal_scales(w2s, "picked_scales"))

@@ -18,12 +18,12 @@ PACK = 4
 T = 2048
 S = 512
 LIST_ROWS = 16
+QUADRANT = 32
 FLOPS = 2 * 2 * 512 * 512 * 512
 
 HALVES = [(0, 256), (256, 256)]
-Z_CHUNKS = [(0, 256), (256, 128), (384, 128)]
-OUT_CHUNKS = [(0, 256), (256, 128), (384, 128)]
-EARLY_N3 = (0, 1, 2, 3)
+CHUNKS = [(0, 256), (256, 128), (384, 128)]
+ABS_ON_VECTOR = 2
 
 
 def entries(lists, first, width):
@@ -38,9 +38,13 @@ def words_in_pairs(grouped):
     return grouped[:].rearrange("p (c i) t -> p c t i", i=2)
 
 
+def scale_rows(plane, q):
+    return plane[QUADRANT * q : QUADRANT * q + 4, :].bitcast(I32)
+
+
 def load_scale_rows(queues, plane, scales):
-    for q in range(4):
-        queues[q % len(queues)].dma_start(out=plane[32 * q : 32 * q + 4, :].bitcast(I32), in_=scales[0, 4 * q : 4 * q + 4, :].bitcast(I32))
+    for q, queue in enumerate(queues):
+        queue.dma_start(out=scale_rows(plane, q), in_=scales[0, 4 * q : 4 * q + 4, :].bitcast(I32))
 
 
 def tile_picked_skipcrossbnorm_none_po_kernel(
@@ -55,43 +59,45 @@ def tile_picked_skipcrossbnorm_none_po_kernel(
         n1_sb = sb.tile([P, S // LIST_ROWS], U16, name="n1_sb")
         n2_sb = sb.tile([P, S // LIST_ROWS], U16, name="n2_sb")
         n3_sb = sb.tile([P, S // LIST_ROWS], U16, name="n3_sb")
-        xw = sb.tile([P, T], I32, name="xw", align_bytes=64)
-        xs = sb.tile([P, T], U8, name="xs", align_bytes=64)
-        w1w = sb.tile([P, 2 * S], U8, name="w1w", tag="w_words", align_bytes=64)
-        w1s = sb.tile([P, S], U8, name="w1s", align_bytes=64)
-        w2s = sb.tile([P, S], U8, name="w2s", align_bytes=64)
+        one = sb.tile([P, 1], F32, name="one", tag="x_words", align_bytes=64)
+        x_scales_sb = sb.tile([P, T], U8, name="x_scales_sb", tag="x_scales", align_bytes=64)
+        w1_words_sb = sb.tile([P, 2 * S], U8, name="w1_words_sb", tag="w_bytes", align_bytes=64)
+        w1_scales_sb = sb.tile([P, S], U8, name="w1_scales_sb", tag="w1_scales", align_bytes=64)
         gain = sb.tile([P, PACK], F32, name="gain")
+        minus_one = sb.tile([P, 1], F32, name="minus_one")
         half = sb.tile([P, 1], F32, name="half")
         zero = sb.tile([P, 1], F32, name="zero")
 
-        nc.vector.memset(xs[:].bitcast(I32), 0)
-        nc.gpsimd.memset(w1s[:].bitcast(I32), 0)
+        nc.vector.memset(one[:], 1.0)
+        nc.vector.memset(x_scales_sb[0 : P // 2, :].bitcast(I32), 0)
+        nc.vector.tensor_scalar(out=minus_one[:], in0=one[:], scalar1=-1.0, scalar2=None, op0=ALU.mult)
+        nc.vector.memset(x_scales_sb[P // 2 : P, :].bitcast(I32), 0)
+        nc.vector.memset(w1_scales_sb[:].bitcast(I32), 0)
         nc.vector.memset(half[:], 0.5)
-        nc.vector.memset(w2s[:].bitcast(I32), 0)
+        x_words_sb = sb.tile([P, T], I32, name="x_words_sb", tag="x_words", align_bytes=64)
 
         nc.sync.dma_start(offs_sb[:], offs)
-        nc.sync.dma_start(out=xw[:], in_=x_words[0].rearrange("p n t -> p (n t)").bitcast(I32))
-        nc.scalar.dma_start(out=w1w[:].bitcast(I32), in_=w1_words[0].bitcast(I32))
-        load_scale_rows((nc.scalar, nc.sync), xs, x_scales)
-        load_scale_rows((nc.scalar, nc.sync), w1s, w1_scales)
         nc.sync.dma_start(n1_sb[:], n1)
         nc.sync.dma_start(n3_sb[:], n3)
         nc.sync.dma_start(n2_sb[:], n2)
+        nc.sync.dma_start(out=w1_words_sb[:].bitcast(I32), in_=w1_words[0].bitcast(I32))
+        load_scale_rows((nc.sync, nc.scalar, nc.scalar, nc.scalar), x_scales_sb, x_scales)
+        nc.sync.dma_start(out=x_words_sb[:], in_=x_words[0].rearrange("p n t -> p (n t)").bitcast(I32))
+        load_scale_rows((nc.scalar,) * 4, w1_scales_sb, w1_scales)
         nc.gpsimd.dma_start(out=gain[:], in_=gn.rearrange("(p t) o -> p (t o)", t=PACK))
-        load_scale_rows((nc.sync,), w2s, w2_scales)
 
         nc.scalar.activation(out=zero[:], in_=half[:], func=ACT.Ln, scale=2.0)
 
-        def deal_words(words, name):
-            dealt = sb.tile([P, 2 * S], U8, name=name, align_bytes=64)
+        def deal_words(words, tag):
+            dealt = sb.tile([P, 2 * S], U8, name="dealt_words_" + tag, tag=tag, align_bytes=64)
             nc.vector.tensor_copy(
                 out=dealt[:].rearrange("p (t m b) -> p t m b", t=PACK, b=2),
                 in_=words[:].rearrange("p (m t b) -> p t m b", t=PACK, b=2),
             )
             return dealt
 
-        def deal_scales(scales, name):
-            dealt = sb.tile([P, S], U8, name=name, align_bytes=64)
+        def deal_scales(scales, tag):
+            dealt = sb.tile([P, S], U8, name="dealt_scales_" + tag, tag=tag, align_bytes=64)
             nc.vector.tensor_copy(
                 out=dealt[:].rearrange("p (t m) -> p t m", t=PACK),
                 in_=scales[:].rearrange("p (m t) -> p t m", t=PACK),
@@ -99,157 +105,168 @@ def tile_picked_skipcrossbnorm_none_po_kernel(
             return dealt
 
         def product(bank, weights, t, codes, scales):
+            dealt_words, dealt_scales = weights
             nc.tensor.matmul_mx(
                 out=bank,
-                lhsT=weights[0][:, 2 * P * t : 2 * P * (t + 1)].bitcast(FP4X4),
-                lhsT_scale=weights[1][:, P * t : P * (t + 1)],
+                lhsT=dealt_words[:, 2 * P * t : 2 * P * (t + 1)].bitcast(FP4X4),
+                lhsT_scale=dealt_scales[:, P * t : P * (t + 1)],
                 rhs=codes.bitcast(FP8X4),
                 rhs_scale=scales,
                 start=True,
                 stop=True,
             )
 
-        w1_dealt_words = deal_words(w1w, "w1_dw")
-        w2w = sb.tile([P, 2 * S], U8, name="w2w", tag="w_words", align_bytes=64)
-        nc.sync.dma_start(out=w2w[:].bitcast(I32), in_=w2_words[0].bitcast(I32))
-        xgs = sb.tile([P, S], U8, name="picked_scales", align_bytes=64)
-        xg = sb.tile([P, S], I32, name="picked_words", align_bytes=64)
-        nc.vector.tensor_copy(out=xgs[:], in_=xs[:].indirect(offs_sb[:]))
-        for first, width in HALVES:
+        w1_dealt_words = deal_words(w1_words_sb, "w1_dealt_words")
+        w2_words_sb = sb.tile([P, 2 * S], U8, name="w2_words_sb", tag="w_bytes", align_bytes=64)
+        nc.sync.dma_start(out=w2_words_sb[:].bitcast(I32), in_=w2_words[0].bitcast(I32))
+        picked_scales = sb.tile([P, S], U8, name="picked_scales", align_bytes=64)
+        nc.vector.tensor_copy(out=picked_scales[:], in_=x_scales_sb[:].indirect(offs_sb[:]))
+        w1 = (w1_dealt_words, deal_scales(w1_scales_sb, "w1_dealt_scales"))
+        picked_words = {}
+        for (first, width), tag in zip(HALVES, ("x_scales", "w1_scales")):
+            picked_words[first] = sb.tile([P, width], I32, name="picked_words%d" % first, tag=tag, align_bytes=64)
             nc.vector.tensor_copy(
-                out=xg[:, first : first + width].bitcast(U32),
-                in_=xw[:].bitcast(U32).indirect(entries(offs_sb, first, width)),
+                out=picked_words[first][:].bitcast(U32),
+                in_=x_words_sb[:].bitcast(U32).indirect(entries(offs_sb, first, width)),
             )
-        w1 = (w1_dealt_words, deal_scales(w1s, "w1_ds"))
+        w2_dealt_words = deal_words(w2_words_sb, "x_words")
+        w2_scales_sb = sb.tile([P, S], U8, name="w2_scales_sb", tag="w_bytes", align_bytes=64)
+        nc.gpsimd.memset(w2_scales_sb[:].bitcast(I32), 0)
+        load_scale_rows((nc.sync,) * 4, w2_scales_sb, w2_scales)
 
         y_ps = [ps.tile([P, S], F32, name="y_ps%d" % t, tag="bank%d" % t) for t in range(PACK)]
         for pair in ((0, 1), (2, 3)):
             for first, width in HALVES:
                 for t in pair:
                     cols = slice(first, first + width)
-                    product(y_ps[t][:, cols], w1, t, xg[:, cols], xgs[:, cols])
+                    product(y_ps[t][:, cols], w1, t, picked_words[first][:], picked_scales[:, cols])
 
-        y = [sb.tile([P, S], F32, name="y%d" % t) for t in range(PACK)]
-        size = [sb.tile([P, S], F32, name="size%d" % t) for t in range(PACK)]
+        y_window = [sb.tile([P, 2 * S], F32, name="y%d" % t) for t in range(PACK)]
+        y = [window[:, 0:S] for window in y_window]
+        y_abs = [window[:, S : 2 * S] for window in y_window]
         logs = [sb.tile([P, S], F32, name="logs%d" % t) for t in range(PACK)]
-        for t in range(PACK):
-            nc.scalar.activation(out=size[t][:], in_=y_ps[t][:], func=ACT.Abs, bias=zero[:])
-            nc.vector.tensor_copy(out=y[t][:], in_=y_ps[t][:])
-        for t in range(PACK):
-            nc.scalar.activation(out=logs[t][:], in_=size[t][:], func=ACT.Ln, bias=half[:])
+        on_scalar = [t for t in range(PACK) if t != ABS_ON_VECTOR]
+        nc.vector.tensor_copy(out=y[1], in_=y_ps[1][:])
+        for t in on_scalar:
+            nc.scalar.activation(out=y_abs[t], in_=y_ps[t][:], func=ACT.Abs, bias=zero[:])
+        for t in (0, ABS_ON_VECTOR):
+            nc.vector.tensor_copy(out=y[t], in_=y_ps[t][:])
+        nc.vector.scalar_tensor_tensor(
+            out=y_abs[ABS_ON_VECTOR],
+            in0=y_ps[ABS_ON_VECTOR][:],
+            scalar=minus_one[:],
+            in1=y[ABS_ON_VECTOR],
+            op0=ALU.mult,
+            op1=ALU.max,
+        )
+        nc.vector.tensor_copy(out=y[3], in_=y_ps[3][:])
+        for t in on_scalar + [ABS_ON_VECTOR]:
+            nc.scalar.activation(out=logs[t][:], in_=y_abs[t], func=ACT.Ln, bias=half[:])
 
-        yg = sb.tile([P, PACK, S], F32, name="yg")
+        gained = sb.tile([P, PACK, S], F32, name="gained")
         for t in range(PACK):
             nc.gpsimd.tensor_scalar(
-                out=yg[:, t, :], in0=y[t][:], scalar1=gain[:, t : t + 1], scalar2=0.0, op0=ALU.mult, op1=ALU.add
+                out=gained[:, t, :], in0=y[t], scalar1=gain[:, t : t + 1], scalar2=0.0, op0=ALU.mult, op1=ALU.add
             )
 
-        w2 = (deal_words(w2w, "picked_words"), deal_scales(w2s, "picked_scales"))
+        w2 = (w2_dealt_words, deal_scales(w2_scales_sb, "picked_scales"))
 
-        y3 = sb.tile([P, PACK, S], F32, name="y_at_n3")
+        y_at_n3 = sb.tile([P, PACK, S], F32, name="y_at_n3")
+        for t in (1, 0, 2, 3):
+            nc.vector.tensor_copy(out=y_at_n3[:, t, :], in_=y_window[t][:].indirect(n3_sb[:]))
 
-        def fetch_y3(t):
-            for first, width in HALVES:
-                nc.vector.tensor_copy(
-                    out=y3[:, t, first : first + width], in_=y[t][:].indirect(entries(n3_sb, first, width))
-                )
-
-        inv = sb.tile([P, PACK, S], F32, name="inv")
-        zw = sb.tile([P, S], I32, name="zw", align_bytes=64)
-        zs = sb.tile([P, S], U8, name="zs", align_bytes=64)
+        inverse = sb.tile([P, PACK, S], F32, name="inverse")
+        z_words = sb.tile([P, S], I32, name="z_words", align_bytes=64)
+        z_scales = sb.tile([P, S], U8, name="z_scales", align_bytes=64)
         h = [sb.tile([P, S], F32, name="h%d" % t) for t in range(PACK)]
-        for t in EARLY_N3:
-            fetch_y3(t)
-        for c, (first, width) in enumerate(Z_CHUNKS):
+        for c, (first, width) in enumerate(CHUNKS):
             cols = slice(first, first + width)
             for t in range(PACK):
                 nc.scalar.activation(
-                    out=inv[:, t, cols],
+                    out=inverse[:, t, cols],
                     in_=logs[t][:].indirect(entries(n1_sb, first, width)),
                     func=ACT.Exp,
                     scale=-1.0,
                 )
-            zb = sb.tile([P, width, PACK], BF16, name="zb%d" % c, align_bytes=64)
+            z_grouped = sb.tile([P, width, PACK], BF16, name="z_grouped%d" % c, align_bytes=64)
             nc.vector.tensor_tensor(
-                out=words_in_pairs(zb),
-                in0=planes_in_pairs(yg, first, width),
-                in1=planes_in_pairs(inv, first, width),
+                out=words_in_pairs(z_grouped),
+                in0=planes_in_pairs(gained, first, width),
+                in1=planes_in_pairs(inverse, first, width),
                 op=ALU.mult,
             )
             nc.vector.quantize_mx(
-                out=zw[:, cols].bitcast(FP8X4), scales=zs[:, cols], in_=zb[:].rearrange("p c t -> p (c t)")
+                out=z_words[:, cols].bitcast(FP8X4),
+                scales=z_scales[:, cols],
+                in_=z_grouped[:].rearrange("p c t -> p (c t)"),
             )
 
-        for c, (first, width) in enumerate(Z_CHUNKS):
+        last_chunk = len(CHUNKS) - 1
+        for c, (first, width) in enumerate(CHUNKS):
             cols = slice(first, first + width)
-            if c == 0:
-                pairs = [ps.tile([P, 2, width], F32, name="h_ps0%d" % u, tag="bank%d" % (4 + u)) for u in range(2)]
-                banks = [pairs[t // 2][:, t % 2, :] for t in range(PACK)]
-            elif c == 1:
-                pairs = [ps.tile([P, 2, width], F32, name="h_ps1%d" % u, tag="bank%d" % (6 + u)) for u in range(2)]
+            if c < last_chunk:
+                pairs = [
+                    ps.tile([P, 2, width], F32, name="h_ps%d%d" % (c, u), tag="bank%d" % (PACK + 2 * c + u))
+                    for u in range(2)
+                ]
                 banks = [pairs[t // 2][:, t % 2, :] for t in range(PACK)]
             else:
-                singles = [ps.tile([P, width], F32, name="h_ps2%d" % t, tag="bank%d" % t) for t in range(PACK)]
+                singles = [ps.tile([P, width], F32, name="h_ps%d%d" % (c, t), tag="bank%d" % t) for t in range(PACK)]
                 banks = [single[:] for single in singles]
             for t in range(PACK):
-                product(banks[t], w2, t, zw[:, cols], zs[:, cols])
+                product(banks[t], w2, t, z_words[:, cols], z_scales[:, cols])
             for t in range(PACK):
                 nc.scalar.activation(out=h[t][:, cols], in_=banks[t], func=ACT.Copy, scale=0.75)
 
         left = sb.tile([P, PACK, S], F32, name="left")
         right = sb.tile([P, PACK, S], F32, name="right")
-        res = sb.tile([P, PACK, S], F32, name="res")
-        ow = sb.tile([P, S], I32, name="ow", align_bytes=64)
-        osc = sb.tile([P, S], U8, name="osc", align_bytes=64)
+        result = sb.tile([P, PACK, S], F32, name="result")
+        result_words = sb.tile([P, S], I32, name="result_words", align_bytes=64)
+        result_scales = sb.tile([P, S], U8, name="result_scales", align_bytes=64)
         out_rows = out_0.rearrange("(p t) j -> p t j", t=PACK)
         out_words = out_1[0].rearrange("p n t -> p (n t)").bitcast(I32)
 
-        for first, width in Z_CHUNKS:
+        for first, width in CHUNKS:
             cols = slice(first, first + width)
             for t in range(PACK):
-                if t in EARLY_N3:
-                    fetched = y3[:, t, cols]
-                else:
-                    fetched = y[t][:].indirect(entries(n3_sb, first, width))
-                nc.vector.tensor_tensor(out=left[:, t, cols], in0=fetched, in1=h[t][:, cols], op=ALU.mult)
+                nc.vector.tensor_tensor(out=left[:, t, cols], in0=y_at_n3[:, t, cols], in1=h[t][:, cols], op=ALU.mult)
 
-        waiting = []
-
-        def quantize_out(grouped, cols, queue):
+        def quantize_result(grouped, cols, queue):
             nc.vector.quantize_mx(
-                out=ow[:, cols].bitcast(FP8X4), scales=osc[:, cols], in_=grouped[:].rearrange("p c t -> p (c t)")
+                out=result_words[:, cols].bitcast(FP8X4),
+                scales=result_scales[:, cols],
+                in_=grouped[:].rearrange("p c t -> p (c t)"),
             )
-            queue.dma_start(out=out_words[:, cols], in_=ow[:, cols])
+            queue.dma_start(out=out_words[:, cols], in_=result_words[:, cols])
 
-        for c, (first, width) in enumerate(OUT_CHUNKS):
+        to_quantize = []
+        for c, (first, width) in enumerate(CHUNKS):
             cols = slice(first, first + width)
-            last = c == len(OUT_CHUNKS) - 1
             for t in range(PACK):
                 nc.vector.tensor_tensor(
                     out=right[:, t, cols],
                     in0=h[t][:].indirect(entries(n2_sb, first, width)),
-                    in1=y[t][:, cols],
+                    in1=y_window[t][:, cols],
                     op=ALU.mult,
                 )
-            for grouped, earlier in waiting:
-                quantize_out(grouped, earlier, nc.sync)
-            waiting.clear()
-            ob = sb.tile([P, width, PACK], BF16, name="ob%d" % c, align_bytes=64)
-            if last:
+            for grouped, earlier_cols in to_quantize:
+                quantize_result(grouped, earlier_cols, nc.sync)
+            to_quantize.clear()
+            result_grouped = sb.tile([P, width, PACK], BF16, name="result_grouped%d" % c, align_bytes=64)
+            if c == last_chunk:
                 nc.vector.tensor_tensor(
-                    out=words_in_pairs(ob),
+                    out=words_in_pairs(result_grouped),
                     in0=planes_in_pairs(left, first, width),
                     in1=planes_in_pairs(right, first, width),
                     op=ALU.subtract,
                 )
-                quantize_out(ob, cols, nc.scalar)
-                for q in range(4):
-                    queue = nc.scalar if q % 2 else nc.sync
-                    queue.dma_start(
-                        out=out_2[0, 4 * q : 4 * q + 4, :].bitcast(I32), in_=osc[32 * q : 32 * q + 4, :].bitcast(I32)
-                    )
-            nc.vector.tensor_tensor(out=res[:, :, cols], in0=left[:, :, cols], in1=right[:, :, cols], op=ALU.subtract)
-            nc.sync.dma_start(out=out_rows[:, :, cols], in_=res[:, :, cols])
-            if not last:
-                nc.scalar.copy(out=words_in_pairs(ob), in_=planes_in_pairs(res, first, width))
-                waiting.append((ob, cols))
+                quantize_result(result_grouped, cols, nc.scalar)
+                for q, queue in enumerate((nc.sync, nc.scalar, nc.sync, nc.scalar)):
+                    queue.dma_start(out=out_2[0, 4 * q : 4 * q + 4, :].bitcast(I32), in_=scale_rows(result_scales, q))
+            nc.vector.tensor_tensor(
+                out=result[:, :, cols], in0=left[:, :, cols], in1=right[:, :, cols], op=ALU.subtract
+            )
+            nc.sync.dma_start(out=out_rows[:, :, cols], in_=result[:, :, cols])
+            if c < last_chunk:
+                nc.scalar.copy(out=words_in_pairs(result_grouped), in_=planes_in_pairs(result, first, width))
+                to_quantize.append((result_grouped, cols))

from contextlib import ExitStack

import concourse.mybir as mybir

F32 = mybir.dt.float32
BF16 = mybir.dt.bfloat16
I32 = mybir.dt.int32
U32 = mybir.dt.uint32
U16 = mybir.dt.uint16
U8 = mybir.dt.uint8
FP8X4 = mybir.dt.float8_e4m3fn_x4
FP4X4 = mybir.dt.float4_e2m1fn_x4
ACT = mybir.ActivationFunctionType
ALU = mybir.AluOpType

P = 128
PACK = 4
T = 2048
S = 512
LIST_ROWS = 16
QUADRANT = 32
FLOPS = 2 * 2 * 512 * 512 * 512

HALVES = [(0, 256), (256, 256)]
CHUNKS = [(0, 256), (256, 128), (384, 128)]
ABS_ON_VECTOR = 2


def entries(lists, first, width):
    return lists[:, first // LIST_ROWS : (first + width) // LIST_ROWS]


def planes_in_pairs(planes, first, width):
    return planes[:, :, first : first + width].rearrange("p t (c i) -> p c t i", i=2)


def words_in_pairs(grouped):
    return grouped[:].rearrange("p (c i) t -> p c t i", i=2)


def scale_rows(plane, q):
    return plane[QUADRANT * q : QUADRANT * q + 4, :].bitcast(I32)


def load_scale_rows(queues, plane, scales):
    for q, queue in enumerate(queues):
        queue.dma_start(out=scale_rows(plane, q), in_=scales[0, 4 * q : 4 * q + 4, :].bitcast(I32))


def tile_picked_skipcrossbnorm_none_po_kernel(
    tc, x_words, x_scales, w1_words, w1_scales, gn, w2_words, w2_scales, offs, n1, n2, n3, out_0, out_1, out_2
):
    nc = tc.nc
    with ExitStack() as ctx:
        sb = ctx.enter_context(tc.tile_pool(name="sb", bufs=1))
        ps = ctx.enter_context(tc.psum_pool(name="ps", bufs=1))

        offs_sb = sb.tile([P, S // LIST_ROWS], U16, name="offs_sb")
        n1_sb = sb.tile([P, S // LIST_ROWS], U16, name="n1_sb")
        n2_sb = sb.tile([P, S // LIST_ROWS], U16, name="n2_sb")
        n3_sb = sb.tile([P, S // LIST_ROWS], U16, name="n3_sb")
        one = sb.tile([P, 1], F32, name="one", tag="x_words", align_bytes=64)
        x_scales_sb = sb.tile([P, T], U8, name="x_scales_sb", tag="x_scales", align_bytes=64)
        w1_words_sb = sb.tile([P, 2 * S], U8, name="w1_words_sb", tag="w_bytes", align_bytes=64)
        w1_scales_sb = sb.tile([P, S], U8, name="w1_scales_sb", tag="w1_scales", align_bytes=64)
        gain = sb.tile([P, PACK], F32, name="gain")
        minus_one = sb.tile([P, 1], F32, name="minus_one")
        half = sb.tile([P, 1], F32, name="half")
        zero = sb.tile([P, 1], F32, name="zero")

        nc.vector.memset(one[:], 1.0)
        nc.vector.memset(x_scales_sb[0 : P // 2, :].bitcast(I32), 0)
        nc.vector.tensor_scalar(out=minus_one[:], in0=one[:], scalar1=-1.0, scalar2=None, op0=ALU.mult)
        nc.vector.memset(x_scales_sb[P // 2 : P, :].bitcast(I32), 0)
        nc.vector.memset(w1_scales_sb[:].bitcast(I32), 0)
        nc.vector.memset(half[:], 0.5)
        x_words_sb = sb.tile([P, T], I32, name="x_words_sb", tag="x_words", align_bytes=64)

        nc.sync.dma_start(offs_sb[:], offs)
        nc.sync.dma_start(n1_sb[:], n1)
        nc.sync.dma_start(n3_sb[:], n3)
        nc.sync.dma_start(n2_sb[:], n2)
        nc.sync.dma_start(out=w1_words_sb[:].bitcast(I32), in_=w1_words[0].bitcast(I32))
        load_scale_rows((nc.sync, nc.scalar, nc.scalar, nc.scalar), x_scales_sb, x_scales)
        nc.sync.dma_start(out=x_words_sb[:], in_=x_words[0].rearrange("p n t -> p (n t)").bitcast(I32))
        load_scale_rows((nc.scalar,) * 4, w1_scales_sb, w1_scales)
        nc.gpsimd.dma_start(out=gain[:], in_=gn.rearrange("(p t) o -> p (t o)", t=PACK))

        nc.scalar.activation(out=zero[:], in_=half[:], func=ACT.Ln, scale=2.0)

        def deal_words(words, tag):
            dealt = sb.tile([P, 2 * S], U8, name="dealt_words_" + tag, tag=tag, align_bytes=64)
            nc.vector.tensor_copy(
                out=dealt[:].rearrange("p (t m b) -> p t m b", t=PACK, b=2),
                in_=words[:].rearrange("p (m t b) -> p t m b", t=PACK, b=2),
            )
            return dealt

        def deal_scales(scales, tag):
            dealt = sb.tile([P, S], U8, name="dealt_scales_" + tag, tag=tag, align_bytes=64)
            nc.vector.tensor_copy(
                out=dealt[:].rearrange("p (t m) -> p t m", t=PACK),
                in_=scales[:].rearrange("p (m t) -> p t m", t=PACK),
            )
            return dealt

        def product(bank, weights, t, codes, scales):
            dealt_words, dealt_scales = weights
            nc.tensor.matmul_mx(
                out=bank,
                lhsT=dealt_words[:, 2 * P * t : 2 * P * (t + 1)].bitcast(FP4X4),
                lhsT_scale=dealt_scales[:, P * t : P * (t + 1)],
                rhs=codes.bitcast(FP8X4),
                rhs_scale=scales,
                start=True,
                stop=True,
            )

        w1_dealt_words = deal_words(w1_words_sb, "w1_dealt_words")
        w2_words_sb = sb.tile([P, 2 * S], U8, name="w2_words_sb", tag="w_bytes", align_bytes=64)
        nc.sync.dma_start(out=w2_words_sb[:].bitcast(I32), in_=w2_words[0].bitcast(I32))
        picked_scales = sb.tile([P, S], U8, name="picked_scales", align_bytes=64)
        nc.vector.tensor_copy(out=picked_scales[:], in_=x_scales_sb[:].indirect(offs_sb[:]))
        w1 = (w1_dealt_words, deal_scales(w1_scales_sb, "w1_dealt_scales"))
        picked_words = {}
        for (first, width), tag in zip(HALVES, ("x_scales", "w1_scales")):
            picked_words[first] = sb.tile([P, width], I32, name="picked_words%d" % first, tag=tag, align_bytes=64)
            nc.vector.tensor_copy(
                out=picked_words[first][:].bitcast(U32),
                in_=x_words_sb[:].bitcast(U32).indirect(entries(offs_sb, first, width)),
            )
        w2_dealt_words = deal_words(w2_words_sb, "x_words")
        w2_scales_sb = sb.tile([P, S], U8, name="w2_scales_sb", tag="w_bytes", align_bytes=64)
        nc.gpsimd.memset(w2_scales_sb[:].bitcast(I32), 0)
        load_scale_rows((nc.sync,) * 4, w2_scales_sb, w2_scales)

        y_ps = [ps.tile([P, S], F32, name="y_ps%d" % t, tag="bank%d" % t) for t in range(PACK)]
        for pair in ((0, 1), (2, 3)):
            for first, width in HALVES:
                for t in pair:
                    cols = slice(first, first + width)
                    product(y_ps[t][:, cols], w1, t, picked_words[first][:], picked_scales[:, cols])

        y_window = [sb.tile([P, 2 * S], F32, name="y%d" % t) for t in range(PACK)]
        y = [window[:, 0:S] for window in y_window]
        y_abs = [window[:, S : 2 * S] for window in y_window]
        logs = [sb.tile([P, S], F32, name="logs%d" % t) for t in range(PACK)]
        on_scalar = [t for t in range(PACK) if t != ABS_ON_VECTOR]
        nc.vector.tensor_copy(out=y[1], in_=y_ps[1][:])
        for t in on_scalar:
            nc.scalar.activation(out=y_abs[t], in_=y_ps[t][:], func=ACT.Abs, bias=zero[:])
        for t in (0, ABS_ON_VECTOR):
            nc.vector.tensor_copy(out=y[t], in_=y_ps[t][:])
        nc.vector.scalar_tensor_tensor(
            out=y_abs[ABS_ON_VECTOR],
            in0=y_ps[ABS_ON_VECTOR][:],
            scalar=minus_one[:],
            in1=y[ABS_ON_VECTOR],
            op0=ALU.mult,
            op1=ALU.max,
        )
        nc.vector.tensor_copy(out=y[3], in_=y_ps[3][:])
        for t in on_scalar + [ABS_ON_VECTOR]:
            nc.scalar.activation(out=logs[t][:], in_=y_abs[t], func=ACT.Ln, bias=half[:])

        gained = sb.tile([P, PACK, S], F32, name="gained")
        for t in range(PACK):
            nc.gpsimd.tensor_scalar(
                out=gained[:, t, :], in0=y[t], scalar1=gain[:, t : t + 1], scalar2=0.0, op0=ALU.mult, op1=ALU.add
            )

        w2 = (w2_dealt_words, deal_scales(w2_scales_sb, "picked_scales"))

        y_at_n3 = sb.tile([P, PACK, S], F32, name="y_at_n3")
        for t in (1, 0, 2, 3):
            nc.vector.tensor_copy(out=y_at_n3[:, t, :], in_=y_window[t][:].indirect(n3_sb[:]))

        inverse = sb.tile([P, PACK, S], F32, name="inverse")
        z_words = sb.tile([P, S], I32, name="z_words", align_bytes=64)
        z_scales = sb.tile([P, S], U8, name="z_scales", align_bytes=64)
        h = [sb.tile([P, S], F32, name="h%d" % t) for t in range(PACK)]
        for c, (first, width) in enumerate(CHUNKS):
            cols = slice(first, first + width)
            for t in range(PACK):
                nc.scalar.activation(
                    out=inverse[:, t, cols],
                    in_=logs[t][:].indirect(entries(n1_sb, first, width)),
                    func=ACT.Exp,
                    scale=-1.0,
                )
            z_grouped = sb.tile([P, width, PACK], BF16, name="z_grouped%d" % c, align_bytes=64)
            nc.vector.tensor_tensor(
                out=words_in_pairs(z_grouped),
                in0=planes_in_pairs(gained, first, width),
                in1=planes_in_pairs(inverse, first, width),
                op=ALU.mult,
            )
            nc.vector.quantize_mx(
                out=z_words[:, cols].bitcast(FP8X4),
                scales=z_scales[:, cols],
                in_=z_grouped[:].rearrange("p c t -> p (c t)"),
            )

        last_chunk = len(CHUNKS) - 1
        for c, (first, width) in enumerate(CHUNKS):
            cols = slice(first, first + width)
            if c < last_chunk:
                pairs = [
                    ps.tile([P, 2, width], F32, name="h_ps%d%d" % (c, u), tag="bank%d" % (PACK + 2 * c + u))
                    for u in range(2)
                ]
                banks = [pairs[t // 2][:, t % 2, :] for t in range(PACK)]
            else:
                singles = [ps.tile([P, width], F32, name="h_ps%d%d" % (c, t), tag="bank%d" % t) for t in range(PACK)]
                banks = [single[:] for single in singles]
            for t in range(PACK):
                product(banks[t], w2, t, z_words[:, cols], z_scales[:, cols])
            for t in range(PACK):
                nc.scalar.activation(out=h[t][:, cols], in_=banks[t], func=ACT.Copy, scale=0.75)

        left = sb.tile([P, PACK, S], F32, name="left")
        right = sb.tile([P, PACK, S], F32, name="right")
        result = sb.tile([P, PACK, S], F32, name="result")
        result_words = sb.tile([P, S], I32, name="result_words", align_bytes=64)
        result_scales = sb.tile([P, S], U8, name="result_scales", align_bytes=64)
        out_rows = out_0.rearrange("(p t) j -> p t j", t=PACK)
        out_words = out_1[0].rearrange("p n t -> p (n t)").bitcast(I32)

        for first, width in CHUNKS:
            cols = slice(first, first + width)
            for t in range(PACK):
                nc.vector.tensor_tensor(out=left[:, t, cols], in0=y_at_n3[:, t, cols], in1=h[t][:, cols], op=ALU.mult)

        def quantize_result(grouped, cols, queue):
            nc.vector.quantize_mx(
                out=result_words[:, cols].bitcast(FP8X4),
                scales=result_scales[:, cols],
                in_=grouped[:].rearrange("p c t -> p (c t)"),
            )
            queue.dma_start(out=out_words[:, cols], in_=result_words[:, cols])

        to_quantize = []
        for c, (first, width) in enumerate(CHUNKS):
            cols = slice(first, first + width)
            for t in range(PACK):
                nc.vector.tensor_tensor(
                    out=right[:, t, cols],
                    in0=h[t][:].indirect(entries(n2_sb, first, width)),
                    in1=y_window[t][:, cols],
                    op=ALU.mult,
                )
            for grouped, earlier_cols in to_quantize:
                quantize_result(grouped, earlier_cols, nc.sync)
            to_quantize.clear()
            result_grouped = sb.tile([P, width, PACK], BF16, name="result_grouped%d" % c, align_bytes=64)
            if c == last_chunk:
                nc.vector.tensor_tensor(
                    out=words_in_pairs(result_grouped),
                    in0=planes_in_pairs(left, first, width),
                    in1=planes_in_pairs(right, first, width),
                    op=ALU.subtract,
                )
                quantize_result(result_grouped, cols, nc.scalar)
                for q, queue in enumerate((nc.sync, nc.scalar, nc.sync, nc.scalar)):
                    queue.dma_start(out=out_2[0, 4 * q : 4 * q + 4, :].bitcast(I32), in_=scale_rows(result_scales, q))
            nc.vector.tensor_tensor(
                out=result[:, :, cols], in0=left[:, :, cols], in1=right[:, :, cols], op=ALU.subtract
            )
            nc.sync.dma_start(out=out_rows[:, :, cols], in_=result[:, :, cols])
            if c < last_chunk:
                nc.scalar.copy(out=words_in_pairs(result_grouped), in_=planes_in_pairs(result, first, width))
                to_quantize.append((result_grouped, cols))
